import numpy as np
import ml_dtypes


def mxq(x, axis, fmt="e4m3"):
    dtype, down = {"e4m3": (ml_dtypes.float8_e4m3fn, 7), "e5m2": (ml_dtypes.float8_e5m2, 14)}[fmt]
    v = np.moveaxis(np.asarray(x, np.float32).astype(ml_dtypes.bfloat16).astype(np.float64), axis, -1)
    blocks = v.reshape(v.shape[:-1] + (-1, 32))
    amax = np.abs(blocks).max(-1, keepdims=True)
    byte = np.maximum(np.where(amax > 0, np.frexp(amax)[1] - 1 + 127, 0) - down, 1)
    scale = np.exp2(byte - 127.0)
    codes = (blocks / scale).astype(np.float32).astype(dtype).astype(np.float64)
    return np.moveaxis((codes * scale).reshape(v.shape), -1, axis)


WIDE = False


def mx_kscale(k):
    if not WIDE:
        return np.ones(k)
    levels = np.array([10, -10, 5, -5, 0])
    if k % 512:
        return np.exp2(np.random.permutation(np.resize(levels, k // 32))).repeat(32)
    a = np.empty((k // 512, 16))
    for p in range(k // 512):
        a[p, :8] = np.random.permutation(np.resize(levels, 8))
        for g in range(8):
            far = levels[np.abs(levels - a[p, g]) >= 10]
            a[p, g + 8] = far[np.random.randint(len(far))]
    return np.exp2(a.ravel()).repeat(32)


def f64(x):
    return np.asarray(x).astype(np.float64)


def striped(idx):
    return np.tile(idx.reshape(-1, 16).T, (8, 1)).astype(np.uint16)


def unstriped(offs):
    return offs[:16].T.reshape(-1).astype(np.int64)


def striped8(idx):
    return np.concatenate([x.reshape(-1, 16).T for x in idx]).astype(np.uint16)


def runs(offs, k):
    lists = np.stack([offs[16 * r : 16 * r + 16].T.reshape(-1) for r in range(8)]).astype(np.int64)
    return lists[np.arange(k) % 512 // 64]


def pack_weight(w):
    k, n = w.shape
    w = f64(np.asarray(w, np.float32).astype(ml_dtypes.bfloat16)).reshape(k // 32, 32, n)
    amax = np.abs(w).max(1)
    byte = np.clip(np.where(amax > 0, np.frexp(amax)[1] - 1 + 127 - 7, 1), 1, 254)
    scaled = (w * np.exp2(127.0 - byte)[:, None, :]).reshape(k, n).astype(np.float32)
    words = np.ascontiguousarray(scaled.reshape(k // 512, 128, 4, n).transpose(0, 1, 3, 2)).astype(ml_dtypes.float8_e4m3fn).view(np.uint8)
    return words, np.ascontiguousarray(byte.astype(np.uint8).reshape(k // 512, 16, n))


def unpack_weight(words, scales):
    g, p, n, _ = words.shape
    vals = np.ascontiguousarray(words).view(ml_dtypes.float8_e4m3fn).astype(np.float64) * np.repeat(np.exp2(scales.astype(np.float64) - 127.0), 8, axis=1)[..., None]
    return vals.transpose(0, 1, 3, 2).reshape(g * 512, n)


def sigmoid(v):
    return 1.0 / (1.0 + np.exp(-np.maximum(v, -700.0)))

def planes(y):
    n, m = y.shape
    v = y.astype(np.float32).astype(ml_dtypes.bfloat16).astype(np.float64).reshape(n // 32, 32, m)
    top = np.abs(v).max(1)
    byte = np.clip(np.where(top > 0, np.frexp(top)[1] - 1 + 127 - 7, 1), 1, 254)
    codes = (v * np.exp2(127.0 - byte)[:, None, :]).reshape(n, m).astype(np.float32).astype(ml_dtypes.float8_e4m3fn).view(np.uint8)
    words = codes.reshape(n // 512, 128, 4, m).transpose(0, 1, 3, 2)
    return np.ascontiguousarray(words), np.ascontiguousarray(byte.astype(np.uint8).reshape(n // 512, 16, m))


K, T, S, N, H = 512, 2048, 512, 512, 512


def setup_inputs():
    n = np.random.standard_normal
    s = mx_kscale(K)[:, None]
    u = mx_kscale(H)
    packed_xT = pack_weight(n((K, T)) * s)
    packed_w1 = pack_weight(n((K, H)) / np.sqrt(K) / s)
    packed_w2 = pack_weight(n((H, N)) / np.sqrt(H) / u[:, None])
    return {
        "x_words": packed_xT[0],
        "x_scales": packed_xT[1],
        "w1_words": packed_w1[0],
        "w1_scales": packed_w1[1],
        "gn": (np.random.uniform(0.5, 1.5, (H, 1)) * u[:, None]).astype(np.float32),
        "w2_words": packed_w2[0],
        "w2_scales": packed_w2[1],
        "offs": striped(np.random.permutation(T)[:S]),
        "n1": striped8(np.stack([np.random.permutation(S) for _ in range(8)])),
        "n2": striped8(np.stack([np.random.permutation(S) for _ in range(8)])),
        "n3": striped8(np.stack([np.random.permutation(S) for _ in range(8)])),
        "n4": striped8(np.stack([np.random.permutation(S) for _ in range(8)])),
    }


def reference(x_words, x_scales, w1_words, w1_scales, gn, w2_words, w2_scales, offs, n1, n2, n3, n4):
    xq = unpack_weight(x_words, x_scales)[:, unstriped(offs)]
    y = unpack_weight(w1_words, w1_scales).T @ xq
    th = np.tanh(y)
    z = f64(gn) * (th * (th[np.arange(H)[:, None], runs(n1, H)]) - (0.5 * (th[np.arange(H)[:, None], runs(n2, H)])))
    h = unpack_weight(w2_words, w2_scales).T @ mxq(z, 0, "e4m3")
    a = h[np.arange(N)[:, None], runs(n3, N)]
    b = h[np.arange(N)[:, None], runs(n4, N)]
    out_0 = h + sigmoid(a - b) * (b - h)
    return (out_0,) + planes(out_0)

@@ -1,0 +1,268 @@
+from contextlib import ExitStack
+
+import concourse.mybir as mybir
+
+K, T, S, H, N = 512, 2048, 512, 512, 512
+FLOPS = 2 * K * H * S + 2 * H * N * S
+
+F32 = mybir.dt.float32
+BF16 = mybir.dt.bfloat16
+I32 = mybir.dt.int32
+U32 = mybir.dt.uint32
+U16 = mybir.dt.uint16
+U8 = mybir.dt.uint8
+FP8X4 = mybir.dt.float8_e4m3fn_x4
+ACT = mybir.ActivationFunctionType
+ALU = mybir.AluOpType
+
+P = 128
+PACK = 4
+LIST = 16
+HALVES = [(0, 256), (256, 512)]
+CHUNKS = [(0, 256), (256, 384), (384, 512)]
+
+
+def tile_picked_tanmix_none_po_kernel(
+    tc, x_words, x_scales, w1_words, w1_scales, gn, w2_words, w2_scales, offs, n1, n2, n3, n4, out_0, out_1, out_2
+):
+    nc = tc.nc
+
+    def words_of(ap):
+        return ap[0].rearrange("p n t -> p (n t)").bitcast(I32)
+
+    def load_scales(queue, plane, scales, quadrants):
+        for q in quadrants:
+            queue.dma_start(out=plane[32 * q : 32 * q + 4, :].bitcast(I32), in_=scales[0, 4 * q : 4 * q + 4, :].bitcast(I32))
+
+    def picks(window, offsets, a, b):
+        return window[:].indirect(offsets[:, a // LIST : b // LIST])
+
+    def woven(engine_copy, dst, src):
+        engine_copy(
+            out=dst[:].rearrange("p (c i t) -> p c t i", i=4, t=PACK),
+            in_=src[:].rearrange("p t (c i) -> p c t i", i=4),
+        )
+
+    with ExitStack() as ctx:
+        keep = ctx.enter_context(tc.tile_pool(name="keep", bufs=1))
+        late = ctx.enter_context(tc.tile_pool(name="late", bufs=1))
+        psum = ctx.enter_context(tc.psum_pool(name="psum", bufs=1))
+
+        lists = [keep.tile([P, S // LIST], U16, name="list%d" % i) for i in range(5)]
+        l_offs, l1, l2, l3, l4 = lists
+        xw = late.tile([P, T], I32, name="xw", align_bytes=64, offset=0)
+        xs = keep.tile([P, T], U8, name="xs", align_bytes=64)
+        w1w = keep.tile([P, H], I32, name="w1w", align_bytes=64)
+        w1s = keep.tile([P, H], U8, name="w1s", align_bytes=64)
+        w2w = keep.tile([P, N], I32, name="w2w", align_bytes=64)
+        w2s = keep.tile([P, N], U8, name="w2s", align_bytes=64)
+        gain = keep.tile([P, PACK], F32, name="gain")
+        warm = keep.tile([P, 8], F32, name="warm")
+
+        nc.vector.memset(xs[:].bitcast(I32), 0)
+        nc.gpsimd.memset(w1s[:].bitcast(I32), 0)
+        nc.gpsimd.memset(w2s[:].bitcast(I32), 0)
+        nc.vector.memset(warm[:], 0.0)
+
+        nc.sync.dma_start(out=l_offs[:], in_=offs)
+        nc.sync.dma_start(out=w1w[:], in_=words_of(w1_words))
+        nc.sync.dma_start(out=xw[:], in_=words_of(x_words))
+        load_scales(nc.scalar, xs, x_scales, range(4))
+        load_scales(nc.scalar, w1s, w1_scales, range(1))
+        load_scales(nc.gpsimd, w1s, w1_scales, range(1, 4))
+        load_scales(nc.gpsimd, w2s, w2_scales, range(4))
+        nc.scalar.activation(out=warm[:, 1:2], in_=warm[:, 0:1], func=ACT.Sigmoid)
+        nc.sync.dma_start(out=gain[:], in_=gn.rearrange("(p t) o -> p (t o)", t=PACK))
+        nc.sync.dma_start(out=w2w[:], in_=words_of(w2_words))
+        for tile, src in ((l1, n1), (l2, n2), (l3, n3), (l4, n4)):
+            nc.sync.dma_start(out=tile[:], in_=src)
+
+        def deal(dst, src):
+            nc.vector.tensor_copy(
+                out=dst[:].rearrange("p (t m) -> p m t", t=PACK), in_=src[:].rearrange("p (m t) -> p m t", t=PACK)
+            )
+
+        def product(bank, w, t, codes, scales):
+            cols = slice(t * P, (t + 1) * P)
+            nc.tensor.matmul_mx(
+                out=bank, lhsT=w[0][:, cols].bitcast(FP8X4), lhsT_scale=w[1][:, cols],
+                rhs=codes.bitcast(FP8X4), rhs_scale=scales, start=True, stop=True,
+            )
+
+        gw = keep.tile([P, S], U32, name="gw", align_bytes=64)
+        gs = keep.tile([P, S], U8, name="gs", align_bytes=64)
+        nc.vector.tensor_copy(out=gs[:], in_=xs[:].indirect(l_offs[:]))
+        d1w = keep.tile([P, H], I32, name="d1w", align_bytes=64)
+        d1s = keep.tile([P, H], U8, name="d1s", align_bytes=64)
+        deal(d1w, w1w)
+        deal(d1s, w1s)
+        w1 = (d1w, d1s)
+        y = [psum.tile([P, S], F32, name="y%d" % t) for t in range(PACK)]
+        for a, b in HALVES:
+            nc.vector.tensor_copy(out=gw[:, a:b], in_=xw[:].bitcast(U32).indirect(l_offs[:, a // LIST : b // LIST]))
+            for t in range(PACK):
+                product(y[t][:, a:b], w1, t, gw[:, a:b], gs[:, a:b])
+        d2w = late.tile([P, N], I32, name="d2w", align_bytes=64, offset=0)
+        d2s = late.tile([P, N], U8, name="d2s", align_bytes=64, offset=4 * T)
+        deal(d2w, w2w)
+        w2 = (d2w, d2s)
+
+        th = [keep.tile([P, S], F32, name="th%d" % t) for t in range(PACK)]
+        gth = [keep.tile([P, S], F32, name="gth%d" % t) for t in range(PACK)]
+        hth = [keep.tile([P, S], F32, name="hth%d" % t) for t in range(PACK)]
+        prod = [late.tile([P, S], F32, name="prod%d" % t, align_bytes=64, offset=4 * T + 4 * S * t) for t in range(PACK)]
+        zf = [keep.tile([P, PACK, b - a], F32, name="zf%d" % c) for c, (a, b) in enumerate(CHUNKS)]
+        zb = [keep.tile([P, PACK * (b - a)], BF16, name="zb%d" % c, align_bytes=64) for c, (a, b) in enumerate(CHUNKS)]
+        zw = [keep.tile([P, b - a], U32, name="zw%d" % c, align_bytes=64) for c, (a, b) in enumerate(CHUNKS)]
+        zs = [keep.tile([P, b - a], U8, name="zs%d" % c, align_bytes=64) for c, (a, b) in enumerate(CHUNKS)]
+        hp = [psum.tile([P, S], F32, name="hp%d" % t) for t in range(PACK)]
+        h = [keep.tile([P, S], F32, name="h%d" % t) for t in range(PACK)]
+
+        def tables(t, a, b):
+            nc.scalar.activation(out=th[t][:, a:b], in_=y[t][:, a:b], func=ACT.Tanh)
+            nc.scalar.activation(out=gth[t][:, a:b], in_=th[t][:, a:b], func=ACT.Copy, scale=gain[:, t : t + 1])
+            nc.scalar.activation(out=hth[t][:, a:b], in_=gth[t][:, a:b], func=ACT.Copy, scale=-0.5)
+
+        def mix_mul(t, a, b):
+            nc.vector.tensor_tensor(prod[t][:, a:b], picks(th[t], l1, a, b), gth[t][:, a:b], ALU.mult)
+
+        def mix_add(t, c):
+            a, b = CHUNKS[c]
+            nc.vector.tensor_tensor(zf[c][:, t, :], picks(hth[t], l2, a, b), prod[t][:, a:b], ALU.add)
+
+        def round_z(c):
+            woven(nc.vector.tensor_copy if c == len(CHUNKS) - 1 else nc.scalar.copy, zb[c], zf[c])
+
+        def second(c):
+            a, b = CHUNKS[c]
+            nc.vector.quantize_mx(out=zw[c][:].bitcast(FP8X4), scales=zs[c][:], in_=zb[c][:])
+            for t in range(PACK):
+                product(hp[t][:, a:b], w2, t, zw[c][:], zs[c][:])
+
+        def mix(ts, c):
+            a, b = CHUNKS[c]
+            for t in ts:
+                mix_mul(t, a, b)
+            for t in ts:
+                mix_add(t, c)
+
+        for a, b in HALVES:
+            tables(0, a, b)
+        for t in range(1, PACK):
+            tables(t, 0, S)
+        for t in range(2):
+            for a, b in HALVES:
+                mix_mul(t, a, b)
+            for c in range(len(CHUNKS)):
+                mix_add(t, c)
+            if t == 0:
+                deal(d2s, w2s)
+        mix((2, 3), 0)
+        round_z(0)
+        mix((2, 3), 1)
+        round_z(1)
+        second(0)
+        mix((2, 3), 2)
+        second(1)
+        last = CHUNKS[-1][0]
+        nc.scalar.copy(out=h[0][:, :last], in_=hp[0][:, :last])
+        round_z(2)
+        second(2)
+        nc.scalar.copy(out=h[0][:, last:], in_=hp[0][:, last:])
+        for t in range(1, PACK):
+            nc.scalar.copy(out=h[t][:], in_=hp[t][:])
+
+        hb = [keep.tile([P, S], F32, name="hb%d" % t) for t in range(PACK)]
+        diff = [keep.tile([P, S], F32, name="diff%d" % t) for t in range(PACK)]
+        gate = [keep.tile([P, S], F32, name="gate%d" % t) for t in range(PACK)]
+        pull = [keep.tile([P, S], F32, name="pull%d" % t) for t in range(PACK)]
+        step = [keep.tile([P, S], F32, name="step%d" % t) for t in range(PACK)]
+        of = [keep.tile([P, PACK, b - a], F32, name="of%d" % c) for c, (a, b) in enumerate(CHUNKS)]
+        ob = [keep.tile([P, PACK * (b - a)], BF16, name="ob%d" % c, align_bytes=64) for c, (a, b) in enumerate(CHUNKS)]
+        ow = keep.tile([P, S], I32, name="ow", align_bytes=64)
+        osc = keep.tile([P, S], U8, name="osc", align_bytes=64)
+        out_rows = out_0.rearrange("(p t) s -> p t s", t=PACK)
+        out_words = words_of(out_1)
+
+        def fetch(t, a, b):
+            nc.vector.tensor_copy(out=hb[t][:, a:b], in_=picks(h[t], l4, a, b))
+
+        def gates(t, a, b):
+            nc.vector.tensor_tensor(diff[t][:, a:b], picks(h[t], l3, a, b), hb[t][:, a:b], ALU.subtract)
+            nc.scalar.activation(out=gate[t][:, a:b], in_=diff[t][:, a:b], func=ACT.Sigmoid)
+
+        def pulls(t, a, b):
+            nc.vector.tensor_tensor(pull[t][:, a:b], hb[t][:, a:b], hp[t][:, a:b], ALU.subtract)
+
+        def steps(t, a, b):
+            nc.vector.tensor_tensor(step[t][:, a:b], gate[t][:, a:b], pull[t][:, a:b], ALU.mult)
+
+        def land(t, c):
+            a, b = CHUNKS[c]
+            nc.vector.tensor_tensor(of[c][:, t, :], step[t][:, a:b], hp[t][:, a:b], ALU.add)
+
+        def store(c, t0, t1):
+            a, b = CHUNKS[c]
+            nc.sync.dma_start(out=out_rows[:, t0:t1, a:b], in_=of[c][:, t0:t1, :])
+
+        def round_out(c):
+            woven(nc.vector.tensor_copy if c == len(CHUNKS) - 1 else nc.scalar.copy, ob[c], of[c])
+
+        def planes(c):
+            a, b = CHUNKS[c]
+            nc.vector.quantize_mx(out=ow[:, a:b].bitcast(FP8X4), scales=osc[:, a:b], in_=ob[c][:])
+            nc.sync.dma_start(out=out_words[:, a:b], in_=ow[:, a:b])
+
+        def front(items):
+            for t, a, b in items:
+                fetch(t, a, b)
+            for t, a, b in items:
+                gates(t, a, b)
+            for t, a, b in items:
+                pulls(t, a, b)
+
+        for t in range(2):
+            for a, b in HALVES:
+                fetch(t, a, b)
+            if t == 1:
+                steps(0, 0, S)
+            for a, b in HALVES:
+                gates(t, a, b)
+            if t == 1:
+                for c in range(len(CHUNKS)):
+                    land(0, c)
+            pulls(t, 0, S)
+        for c, (a, b) in enumerate(CHUNKS):
+            for t in (2, 3):
+                fetch(t, a, b)
+            if c == 0:
+                steps(1, 0, S)
+            else:
+                for t in (2, 3):
+                    steps(t, *CHUNKS[c - 1])
+            for t in (2, 3):
+                gates(t, a, b)
+            if c == 0:
+                for k in range(len(CHUNKS)):
+                    land(1, k)
+                    store(k, 0, 2)
+            else:
+                for t in (2, 3):
+                    land(t, c - 1)
+                store(c - 1, 2, 4)
+                round_out(c - 1)
+            for t in (2, 3):
+                pulls(t, a, b)
+            if c == 2:
+                planes(0)
+        c = len(CHUNKS) - 1
+        for t in (2, 3):
+            steps(t, *CHUNKS[c])
+        for t in (2, 3):
+            land(t, c)
+        store(c, 2, 4)
+        planes(c - 1)
+        round_out(c)
+        planes(c)
+        for q in range(4):
+            nc.scalar.dma_start(out=out_2[0, 4 * q : 4 * q + 4, :].bitcast(I32), in_=osc[32 * q : 32 * q + 4, :].bitcast(I32))

@@ -32,7 +32,8 @@ def tile_picked_tanmix_none_po_kernel(
 
     def load_scales(queue, plane, scales, quadrants):
         for q in quadrants:
-            queue.dma_start(out=plane[32 * q : 32 * q + 4, :].bitcast(I32), in_=scales[0, 4 * q : 4 * q + 4, :].bitcast(I32))
+            rows = scales[0, 4 * q : 4 * q + 4, :].bitcast(I32)
+            queue.dma_start(out=plane[32 * q : 32 * q + 32, :].bitcast(I32), in_=rows.unsqueeze(0).to_broadcast([8] + list(rows.shape)))
 
     def picks(window, offsets, a, b):
         return window[:].indirect(offsets[:, a // LIST : b // LIST])
@@ -40,7 +41,7 @@ def tile_picked_tanmix_none_po_kernel(
     def woven(engine_copy, dst, src):
         engine_copy(
             out=dst[:].rearrange("p (c i t) -> p c t i", i=4, t=PACK),
-            in_=src[:].rearrange("p t (c i) -> p c t i", i=4),
+            in_=src.rearrange("p t (c i) -> p c t i", i=4),
         )
 
     with ExitStack() as ctx:
@@ -59,23 +60,21 @@ def tile_picked_tanmix_none_po_kernel(
         gain = keep.tile([P, PACK], F32, name="gain")
         warm = keep.tile([P, 8], F32, name="warm")
 
-        nc.vector.memset(xs[:].bitcast(I32), 0)
-        nc.gpsimd.memset(w1s[:].bitcast(I32), 0)
-        nc.gpsimd.memset(w2s[:].bitcast(I32), 0)
         nc.vector.memset(warm[:], 0.0)
+        nc.scalar.activation(out=warm[:, 1:2], in_=warm[:, 0:1], func=ACT.Sigmoid)
 
         nc.sync.dma_start(out=l_offs[:], in_=offs)
+        load_scales(nc.sync, xs, x_scales, range(4))
         nc.sync.dma_start(out=w1w[:], in_=words_of(w1_words))
         nc.sync.dma_start(out=xw[:], in_=words_of(x_words))
-        load_scales(nc.scalar, xs, x_scales, range(4))
-        load_scales(nc.scalar, w1s, w1_scales, range(1))
-        load_scales(nc.gpsimd, w1s, w1_scales, range(1, 4))
-        load_scales(nc.gpsimd, w2s, w2_scales, range(4))
-        nc.scalar.activation(out=warm[:, 1:2], in_=warm[:, 0:1], func=ACT.Sigmoid)
+        load_scales(nc.sync, w1s, w1_scales, range(4))
         nc.sync.dma_start(out=gain[:], in_=gn.rearrange("(p t) o -> p (t o)", t=PACK))
+        nc.sync.dma_start(out=l1[:], in_=n1)
         nc.sync.dma_start(out=w2w[:], in_=words_of(w2_words))
-        for tile, src in ((l1, n1), (l2, n2), (l3, n3), (l4, n4)):
-            nc.sync.dma_start(out=tile[:], in_=src)
+        nc.sync.dma_start(out=l2[:], in_=n2)
+        load_scales(nc.sync, w2s, w2_scales, range(4))
+        nc.sync.dma_start(out=l4[:], in_=n4)
+        nc.sync.dma_start(out=l3[:], in_=n3)
 
         def deal(dst, src):
             nc.vector.tensor_copy(
@@ -103,35 +102,48 @@ def tile_picked_tanmix_none_po_kernel(
             for t in range(PACK):
                 product(y[t][:, a:b], w1, t, gw[:, a:b], gs[:, a:b])
         d2w = late.tile([P, N], I32, name="d2w", align_bytes=64, offset=0)
-        d2s = late.tile([P, N], U8, name="d2s", align_bytes=64, offset=4 * T)
+        d2s = late.tile([P, N], U8, name="d2s", align_bytes=64, offset=4 * T + 8 * S)
         deal(d2w, w2w)
         w2 = (d2w, d2s)
 
-        th = [keep.tile([P, S], F32, name="th%d" % t) for t in range(PACK)]
-        gth = [keep.tile([P, S], F32, name="gth%d" % t) for t in range(PACK)]
+        thw = [keep.tile([P, 2 * S], F32, name="thw%d" % t) for t in range(PACK)]
+        gth_last = late.tile([P, 2 * S + N // 4], F32, name="gth_last", align_bytes=64, offset=4 * T)
+        th = [w[:, :S] for w in thw]
+        gth = [w[:, S:] for w in thw[1:]] + [gth_last[:, :S]]
+        nc.vector.memset(thw[0][:, S:], 0.0)
         hth = [keep.tile([P, S], F32, name="hth%d" % t) for t in range(PACK)]
-        prod = [late.tile([P, S], F32, name="prod%d" % t, align_bytes=64, offset=4 * T + 4 * S * t) for t in range(PACK)]
-        zf = [keep.tile([P, PACK, b - a], F32, name="zf%d" % c) for c, (a, b) in enumerate(CHUNKS)]
-        zb = [keep.tile([P, PACK * (b - a)], BF16, name="zb%d" % c, align_bytes=64) for c, (a, b) in enumerate(CHUNKS)]
+        prod = [keep.tile([P, S], F32, name="prod%d" % t) for t in range(PACK)]
+        at_zb = 4 * T + 8 * S + N
+        zf = [
+            keep.tile([P, PACK, 256], F32, name="zf0"),
+            late.tile([P, PACK, 128], F32, name="zf1", align_bytes=64, offset=4 * T),
+            late.tile([P, PACK, 128], F32, name="zf2", align_bytes=64, offset=at_zb),
+        ]
+        zb = [late.tile([P, PACK * 256], BF16, name="zb0", align_bytes=64, offset=at_zb)] + [
+            keep.tile([P, PACK * 128], BF16, name="zb%d" % c, align_bytes=64) for c in (1, 2)
+        ]
         zw = [keep.tile([P, b - a], U32, name="zw%d" % c, align_bytes=64) for c, (a, b) in enumerate(CHUNKS)]
         zs = [keep.tile([P, b - a], U8, name="zs%d" % c, align_bytes=64) for c, (a, b) in enumerate(CHUNKS)]
         hp = [psum.tile([P, S], F32, name="hp%d" % t) for t in range(PACK)]
-        h = [keep.tile([P, S], F32, name="h%d" % t) for t in range(PACK)]
+        hw = [keep.tile([P, 2 * S if t < PACK - 1 else S], F32, name="hw%d" % t) for t in range(PACK)]
+        h = [w[:, :S] for w in hw]
+        nc.vector.memset(hw[0][:, S:], 0.0)
 
-        def tables(t, a, b):
-            nc.scalar.activation(out=th[t][:, a:b], in_=y[t][:, a:b], func=ACT.Tanh)
-            nc.scalar.activation(out=gth[t][:, a:b], in_=th[t][:, a:b], func=ACT.Copy, scale=gain[:, t : t + 1])
-            nc.scalar.activation(out=hth[t][:, a:b], in_=gth[t][:, a:b], func=ACT.Copy, scale=-0.5)
+        def tables(t, parts):
+            for a, b in parts:
+                nc.scalar.activation(out=th[t][:, a:b], in_=y[t][:, a:b], func=ACT.Tanh)
+                nc.scalar.activation(out=gth[t][:, a:b], in_=th[t][:, a:b], func=ACT.Copy, scale=gain[:, t : t + 1])
+            nc.scalar.activation(out=hth[t][:], in_=gth[t], func=ACT.Copy, scale=-0.5)
 
         def mix_mul(t, a, b):
-            nc.vector.tensor_tensor(prod[t][:, a:b], picks(th[t], l1, a, b), gth[t][:, a:b], ALU.mult)
+            nc.vector.tensor_tensor(prod[t][:, a:b], picks(thw[t], l1, a, b), gth[t][:, a:b], ALU.mult)
 
         def mix_add(t, c):
             a, b = CHUNKS[c]
             nc.vector.tensor_tensor(zf[c][:, t, :], picks(hth[t], l2, a, b), prod[t][:, a:b], ALU.add)
 
         def round_z(c):
-            woven(nc.vector.tensor_copy if c == len(CHUNKS) - 1 else nc.scalar.copy, zb[c], zf[c])
+            woven(nc.vector.tensor_copy if c == len(CHUNKS) - 1 else nc.scalar.copy, zb[c], zf[c][:])
 
         def second(c):
             a, b = CHUNKS[c]
@@ -139,30 +151,25 @@ def tile_picked_tanmix_none_po_kernel(
             for t in range(PACK):
                 product(hp[t][:, a:b], w2, t, zw[c][:], zs[c][:])
 
-        def mix(ts, c):
-            a, b = CHUNKS[c]
-            for t in ts:
-                mix_mul(t, a, b)
-            for t in ts:
-                mix_add(t, c)
-
-        for a, b in HALVES:
-            tables(0, a, b)
-        for t in range(1, PACK):
-            tables(t, 0, S)
-        for t in range(2):
-            for a, b in HALVES:
-                mix_mul(t, a, b)
-            for c in range(len(CHUNKS)):
-                mix_add(t, c)
+        for t in range(PACK):
+            tables(t, HALVES if t == 0 else [(0, S)])
+        for t in range(PACK):
             if t == 0:
-                deal(d2s, w2s)
-        mix((2, 3), 0)
+                for a, b in HALVES:
+                    mix_mul(t, a, b)
+            else:
+                mix_mul(t, 0, S)
+            if t > 0:
+                mix_add(t - 1, 0)
+        mix_add(PACK - 1, 0)
         round_z(0)
-        mix((2, 3), 1)
+        deal(d2s, w2s)
+        for t in range(PACK):
+            mix_add(t, 1)
         round_z(1)
         second(0)
-        mix((2, 3), 2)
+        for t in range(PACK):
+            mix_add(t, 2)
         second(1)
         last = CHUNKS[-1][0]
         nc.scalar.copy(out=h[0][:, :last], in_=hp[0][:, :last])
@@ -170,14 +177,16 @@ def tile_picked_tanmix_none_po_kernel(
         second(2)
         nc.scalar.copy(out=h[0][:, last:], in_=hp[0][:, last:])
         for t in range(1, PACK):
-            nc.scalar.copy(out=h[t][:], in_=hp[t][:])
+            nc.scalar.copy(out=h[t], in_=hp[t][:])
 
-        hb = [keep.tile([P, S], F32, name="hb%d" % t) for t in range(PACK)]
+        hb_rest = [keep.tile([P, S], F32, name="hb%d" % t) for t in range(2)]
+        hb = [hw[1][:, S:], hw[2][:, S:], hb_rest[0][:], hb_rest[1][:]]
+        ha = [keep.tile([P, S], F32, name="ha%d" % t) for t in range(PACK - 1)]
         diff = [keep.tile([P, S], F32, name="diff%d" % t) for t in range(PACK)]
         gate = [keep.tile([P, S], F32, name="gate%d" % t) for t in range(PACK)]
         pull = [keep.tile([P, S], F32, name="pull%d" % t) for t in range(PACK)]
         step = [keep.tile([P, S], F32, name="step%d" % t) for t in range(PACK)]
-        of = [keep.tile([P, PACK, b - a], F32, name="of%d" % c) for c, (a, b) in enumerate(CHUNKS)]
+        of = keep.tile([P, PACK, S], F32, name="of")
         ob = [keep.tile([P, PACK * (b - a)], BF16, name="ob%d" % c, align_bytes=64) for c, (a, b) in enumerate(CHUNKS)]
         ow = keep.tile([P, S], I32, name="ow", align_bytes=64)
         osc = keep.tile([P, S], U8, name="osc", align_bytes=64)
@@ -185,10 +194,10 @@ def tile_picked_tanmix_none_po_kernel(
         out_words = words_of(out_1)
 
         def fetch(t, a, b):
-            nc.vector.tensor_copy(out=hb[t][:, a:b], in_=picks(h[t], l4, a, b))
+            nc.vector.tensor_copy(out=hb[t][:, a:b], in_=picks(hw[t], l4, a, b))
 
         def gates(t, a, b):
-            nc.vector.tensor_tensor(diff[t][:, a:b], picks(h[t], l3, a, b), hb[t][:, a:b], ALU.subtract)
+            nc.vector.tensor_tensor(diff[t][:, a:b], picks(hw[t], l3, a, b), hb[t][:, a:b], ALU.subtract)
             nc.scalar.activation(out=gate[t][:, a:b], in_=diff[t][:, a:b], func=ACT.Sigmoid)
 
         def pulls(t, a, b):
@@ -197,72 +206,73 @@ def tile_picked_tanmix_none_po_kernel(
         def steps(t, a, b):
             nc.vector.tensor_tensor(step[t][:, a:b], gate[t][:, a:b], pull[t][:, a:b], ALU.mult)
 
-        def land(t, c):
-            a, b = CHUNKS[c]
-            nc.vector.tensor_tensor(of[c][:, t, :], step[t][:, a:b], hp[t][:, a:b], ALU.add)
+        def land(t, a, b):
+            nc.vector.tensor_tensor(of[:, t, a:b], step[t][:, a:b], hp[t][:, a:b], ALU.add)
 
-        def store(c, t0, t1):
-            a, b = CHUNKS[c]
-            nc.sync.dma_start(out=out_rows[:, t0:t1, a:b], in_=of[c][:, t0:t1, :])
+        def store(t, a, b):
+            nc.sync.dma_start(out=out_rows[:, t, a:b], in_=of[:, t, a:b])
 
         def round_out(c):
-            woven(nc.vector.tensor_copy if c == len(CHUNKS) - 1 else nc.scalar.copy, ob[c], of[c])
+            a, b = CHUNKS[c]
+            woven(nc.vector.tensor_copy if c == len(CHUNKS) - 1 else nc.scalar.copy, ob[c], of[:, :, a:b])
 
         def planes(c):
             a, b = CHUNKS[c]
             nc.vector.quantize_mx(out=ow[:, a:b].bitcast(FP8X4), scales=osc[:, a:b], in_=ob[c][:])
             nc.sync.dma_start(out=out_words[:, a:b], in_=ow[:, a:b])
 
-        def front(items):
-            for t, a, b in items:
-                fetch(t, a, b)
-            for t, a, b in items:
-                gates(t, a, b)
-            for t, a, b in items:
-                pulls(t, a, b)
+        def fetch_a(t):
+            nc.vector.tensor_copy(out=ha[t][:], in_=picks(hw[t], l3, 0, S))
+            nc.gpsimd.tensor_tensor(diff[t][:], ha[t][:], hb[t], ALU.subtract)
+            nc.scalar.activation(out=gate[t][:], in_=diff[t][:], func=ACT.Sigmoid)
 
-        for t in range(2):
-            for a, b in HALVES:
-                fetch(t, a, b)
-            if t == 1:
-                steps(0, 0, S)
-            for a, b in HALVES:
-                gates(t, a, b)
-            if t == 1:
-                for c in range(len(CHUNKS)):
-                    land(0, c)
+        def steps_g(t):
+            nc.gpsimd.tensor_tensor(step[t][:], gate[t][:], pull[t][:], ALU.mult)
+
+        for t in range(PACK - 1):
+            fetch(t, 0, S)
+            fetch_a(t)
             pulls(t, 0, S)
-        for c, (a, b) in enumerate(CHUNKS):
-            for t in (2, 3):
-                fetch(t, a, b)
-            if c == 0:
-                steps(1, 0, S)
-            else:
-                for t in (2, 3):
-                    steps(t, *CHUNKS[c - 1])
-            for t in (2, 3):
-                gates(t, a, b)
-            if c == 0:
-                for k in range(len(CHUNKS)):
-                    land(1, k)
-                    store(k, 0, 2)
-            else:
-                for t in (2, 3):
-                    land(t, c - 1)
-                store(c - 1, 2, 4)
-                round_out(c - 1)
-            for t in (2, 3):
-                pulls(t, a, b)
-            if c == 2:
-                planes(0)
-        c = len(CHUNKS) - 1
-        for t in (2, 3):
-            steps(t, *CHUNKS[c])
-        for t in (2, 3):
-            land(t, c)
-        store(c, 2, 4)
-        planes(c - 1)
-        round_out(c)
-        planes(c)
+            if t > 0:
+                land(t - 1, 0, S)
+                store(t - 1, 0, S)
+            steps_g(t)
+        t = PACK - 1
+        at_tail = at_zb + 2048
+        tail_step = [late.tile([P, 256], F32, name="ts0", align_bytes=64, offset=at_tail)] + [
+            keep.tile([P, 128], F32, name="ts%d" % c) for c in (1, 2)
+        ]
+        tail_diff = [
+            keep.tile([P, 256], F32, name="td0"),
+            keep.tile([P, 128], F32, name="td1"),
+            late.tile([P, 128], F32, name="td2", align_bytes=64, offset=at_tail),
+        ]
+
+        def tail_gates(c):
+            a, b = CHUNKS[c]
+            nc.vector.tensor_tensor(tail_diff[c][:], picks(hw[t], l3, a, b), hb[t][:, a:b], ALU.subtract)
+            nc.scalar.activation(out=gate[t][:, a:b], in_=tail_diff[c][:], func=ACT.Sigmoid)
+
+        def tail_land(c):
+            a, b = CHUNKS[c]
+            nc.vector.tensor_tensor(tail_step[c][:], gate[t][:, a:b], pull[t][:, a:b], ALU.mult)
+            nc.vector.tensor_tensor(of[:, t, a:b], tail_step[c][:], hp[t][:, a:b], ALU.add)
+            store(t, a, b)
+            round_out(c)
+
+        for a, b in HALVES:
+            fetch(t, a, b)
+        pulls(t, 0, S)
+        tail_gates(0)
+        land(t - 1, 0, S)
+        store(t - 1, 0, S)
+        tail_gates(1)
+        tail_land(0)
+        tail_gates(2)
+        tail_land(1)
+        tail_land(2)
+        planes(0)
+        planes(2)
+        planes(1)
         for q in range(4):
             nc.scalar.dma_start(out=out_2[0, 4 * q : 4 * q + 4, :].bitcast(I32), in_=osc[32 * q : 32 * q + 4, :].bitcast(I32))

@@ -76,9 +76,10 @@ def tile_picked_tanmix_none_po_kernel(
         nc.sync.dma_start(out=l4[:], in_=n4)
         nc.sync.dma_start(out=l3[:], in_=n3)
 
-        def deal(dst, src):
+        def deal(dst, src, line):
             nc.vector.tensor_copy(
-                out=dst[:].rearrange("p (t m) -> p m t", t=PACK), in_=src[:].rearrange("p (m t) -> p m t", t=PACK)
+                out=dst[:].rearrange("p (t c i) -> p c t i", t=PACK, i=line),
+                in_=src[:].rearrange("p (c i t) -> p c t i", t=PACK, i=line),
             )
 
         def product(bank, w, t, codes, scales):
@@ -93,37 +94,35 @@ def tile_picked_tanmix_none_po_kernel(
         nc.vector.tensor_copy(out=gs[:], in_=xs[:].indirect(l_offs[:]))
         d1w = keep.tile([P, H], I32, name="d1w", align_bytes=64)
         d1s = keep.tile([P, H], U8, name="d1s", align_bytes=64)
-        deal(d1w, w1w)
-        deal(d1s, w1s)
+        deal(d1w, w1w, 4)
+        deal(d1s, w1s, 16)
         w1 = (d1w, d1s)
         y = [psum.tile([P, S], F32, name="y%d" % t) for t in range(PACK)]
         for a, b in HALVES:
             nc.vector.tensor_copy(out=gw[:, a:b], in_=xw[:].bitcast(U32).indirect(l_offs[:, a // LIST : b // LIST]))
-            for t in range(PACK):
-                product(y[t][:, a:b], w1, t, gw[:, a:b], gs[:, a:b])
+            product(y[0][:, a:b], w1, 0, gw[:, a:b], gs[:, a:b])
+        for t in range(1, PACK):
+            product(y[t][:], w1, t, gw[:], gs[:])
         d2w = late.tile([P, N], I32, name="d2w", align_bytes=64, offset=0)
-        d2s = late.tile([P, N], U8, name="d2s", align_bytes=64, offset=4 * T + 8 * S)
-        deal(d2w, w2w)
+        d2s = late.tile([P, N], U8, name="d2s", align_bytes=64, offset=4 * T + 4 * S)
+        deal(d2w, w2w, 4)
         w2 = (d2w, d2s)
 
         thw = [keep.tile([P, 2 * S], F32, name="thw%d" % t) for t in range(PACK)]
-        gth_last = late.tile([P, 2 * S + N // 4], F32, name="gth_last", align_bytes=64, offset=4 * T)
+        gth_last = late.tile([P, S + N // 4], F32, name="gth_last", align_bytes=64, offset=4 * T)
         th = [w[:, :S] for w in thw]
         gth = [w[:, S:] for w in thw[1:]] + [gth_last[:, :S]]
         nc.vector.memset(thw[0][:, S:], 0.0)
         hth = [keep.tile([P, S], F32, name="hth%d" % t) for t in range(PACK)]
         prod = [keep.tile([P, S], F32, name="prod%d" % t) for t in range(PACK)]
-        at_zb = 4 * T + 8 * S + N
         zf = [
             keep.tile([P, PACK, 256], F32, name="zf0"),
-            late.tile([P, PACK, 128], F32, name="zf1", align_bytes=64, offset=4 * T),
-            late.tile([P, PACK, 128], F32, name="zf2", align_bytes=64, offset=at_zb),
+            keep.tile([P, PACK, 128], F32, name="zf1"),
+            late.tile([P, PACK, 128], F32, name="zf2", align_bytes=64, offset=4 * T),
         ]
-        zb = [late.tile([P, PACK * 256], BF16, name="zb0", align_bytes=64, offset=at_zb)] + [
-            keep.tile([P, PACK * 128], BF16, name="zb%d" % c, align_bytes=64) for c in (1, 2)
-        ]
-        zw = [keep.tile([P, b - a], U32, name="zw%d" % c, align_bytes=64) for c, (a, b) in enumerate(CHUNKS)]
-        zs = [keep.tile([P, b - a], U8, name="zs%d" % c, align_bytes=64) for c, (a, b) in enumerate(CHUNKS)]
+        zb = [keep.tile([P, PACK * (b - a)], BF16, name="zb%d" % c, align_bytes=64) for c, (a, b) in enumerate(CHUNKS)]
+        zw = keep.tile([P, S], U32, name="zw", align_bytes=64)
+        zs = keep.tile([P, S], U8, name="zs", align_bytes=64)
         hp = [psum.tile([P, S], F32, name="hp%d" % t) for t in range(PACK)]
         hw = [keep.tile([P, 2 * S if t < PACK - 1 else S], F32, name="hw%d" % t) for t in range(PACK)]
         h = [w[:, :S] for w in hw]
@@ -147,9 +146,8 @@ def tile_picked_tanmix_none_po_kernel(
 
         def second(c):
             a, b = CHUNKS[c]
-            nc.vector.quantize_mx(out=zw[c][:].bitcast(FP8X4), scales=zs[c][:], in_=zb[c][:])
-            for t in range(PACK):
-                product(hp[t][:, a:b], w2, t, zw[c][:], zs[c][:])
+            nc.vector.quantize_mx(out=zw[:, a:b].bitcast(FP8X4), scales=zs[:, a:b], in_=zb[c][:])
+            product(hp[0][:, a:b], w2, 0, zw[:, a:b], zs[:, a:b])
 
         for t in range(PACK):
             tables(t, HALVES if t == 0 else [(0, S)])
@@ -159,35 +157,39 @@ def tile_picked_tanmix_none_po_kernel(
                     mix_mul(t, a, b)
             else:
                 mix_mul(t, 0, S)
-            if t > 0:
-                mix_add(t - 1, 0)
-        mix_add(PACK - 1, 0)
-        round_z(0)
-        deal(d2s, w2s)
-        for t in range(PACK):
+            mix_add(t, 0)
             mix_add(t, 1)
+        round_z(0)
         round_z(1)
-        second(0)
+        deal(d2s, w2s, 16)
         for t in range(PACK):
             mix_add(t, 2)
-        second(1)
-        last = CHUNKS[-1][0]
-        nc.scalar.copy(out=h[0][:, :last], in_=hp[0][:, :last])
+        second(0)
         round_z(2)
+        second(1)
         second(2)
-        nc.scalar.copy(out=h[0][:, last:], in_=hp[0][:, last:])
+        nc.scalar.copy(out=h[0], in_=hp[0][:])
         for t in range(1, PACK):
+            product(hp[t][:], w2, t, zw[:], zs[:])
             nc.scalar.copy(out=h[t], in_=hp[t][:])
 
-        hb_rest = [keep.tile([P, S], F32, name="hb%d" % t) for t in range(2)]
+        at_step = 4 * T + 4 * S + N
+        at_pull = at_step + 4 * S
+        hb_rest = [keep.tile([P, S], F32, name="hb2"), late.tile([P, S], F32, name="hb3", align_bytes=64, offset=at_step)]
         hb = [hw[1][:, S:], hw[2][:, S:], hb_rest[0][:], hb_rest[1][:]]
         ha = [keep.tile([P, S], F32, name="ha%d" % t) for t in range(PACK - 1)]
-        diff = [keep.tile([P, S], F32, name="diff%d" % t) for t in range(PACK)]
+        diff = [keep.tile([P, S], F32, name="diff%d" % t) for t in range(PACK - 1)]
         gate = [keep.tile([P, S], F32, name="gate%d" % t) for t in range(PACK)]
-        pull = [keep.tile([P, S], F32, name="pull%d" % t) for t in range(PACK)]
-        step = [keep.tile([P, S], F32, name="step%d" % t) for t in range(PACK)]
+        pull = [
+            late.tile([P, S], F32, name="pull2", align_bytes=64, offset=at_pull) if t == 2 else keep.tile([P, S], F32, name="pull%d" % t)
+            for t in range(PACK)
+        ]
+        step = [
+            late.tile([P, S], F32, name="step1", align_bytes=64, offset=at_step) if t == 1 else keep.tile([P, S], F32, name="step%d" % t)
+            for t in range(PACK - 1)
+        ]
         of = keep.tile([P, PACK, S], F32, name="of")
-        ob = [keep.tile([P, PACK * (b - a)], BF16, name="ob%d" % c, align_bytes=64) for c, (a, b) in enumerate(CHUNKS)]
+        ob = [keep.tile([P, PACK * (b - a)], BF16, name="ob%d" % c, align_bytes=64) for c, (a, b) in enumerate(HALVES)]
         ow = keep.tile([P, S], I32, name="ow", align_bytes=64)
         osc = keep.tile([P, S], U8, name="osc", align_bytes=64)
         out_rows = out_0.rearrange("(p t) s -> p t s", t=PACK)
@@ -196,15 +198,8 @@ def tile_picked_tanmix_none_po_kernel(
         def fetch(t, a, b):
             nc.vector.tensor_copy(out=hb[t][:, a:b], in_=picks(hw[t], l4, a, b))
 
-        def gates(t, a, b):
-            nc.vector.tensor_tensor(diff[t][:, a:b], picks(hw[t], l3, a, b), hb[t][:, a:b], ALU.subtract)
-            nc.scalar.activation(out=gate[t][:, a:b], in_=diff[t][:, a:b], func=ACT.Sigmoid)
-
         def pulls(t, a, b):
             nc.vector.tensor_tensor(pull[t][:, a:b], hb[t][:, a:b], hp[t][:, a:b], ALU.subtract)
-
-        def steps(t, a, b):
-            nc.vector.tensor_tensor(step[t][:, a:b], gate[t][:, a:b], pull[t][:, a:b], ALU.mult)
 
         def land(t, a, b):
             nc.vector.tensor_tensor(of[:, t, a:b], step[t][:, a:b], hp[t][:, a:b], ALU.add)
@@ -213,66 +208,51 @@ def tile_picked_tanmix_none_po_kernel(
             nc.sync.dma_start(out=out_rows[:, t, a:b], in_=of[:, t, a:b])
 
         def round_out(c):
-            a, b = CHUNKS[c]
-            woven(nc.vector.tensor_copy if c == len(CHUNKS) - 1 else nc.scalar.copy, ob[c], of[:, :, a:b])
+            a, b = HALVES[c]
+            woven(nc.vector.tensor_copy if c == len(HALVES) - 1 else nc.scalar.copy, ob[c], of[:, :, a:b])
 
         def planes(c):
-            a, b = CHUNKS[c]
+            a, b = HALVES[c]
             nc.vector.quantize_mx(out=ow[:, a:b].bitcast(FP8X4), scales=osc[:, a:b], in_=ob[c][:])
             nc.sync.dma_start(out=out_words[:, a:b], in_=ow[:, a:b])
 
         def fetch_a(t):
-            nc.vector.tensor_copy(out=ha[t][:], in_=picks(hw[t], l3, 0, S))
-            nc.gpsimd.tensor_tensor(diff[t][:], ha[t][:], hb[t], ALU.subtract)
-            nc.scalar.activation(out=gate[t][:], in_=diff[t][:], func=ACT.Sigmoid)
+            for a, b in HALVES if t < 2 else [(0, S)]:
+                fetch(t, a, b)
+                nc.vector.tensor_copy(out=ha[t][:, a:b], in_=picks(hw[t], l3, a, b))
+            for a, b in HALVES:
+                nc.gpsimd.tensor_tensor(diff[t][:, a:b], ha[t][:, a:b], hb[t][:, a:b], ALU.subtract)
+                nc.scalar.activation(out=gate[t][:, a:b], in_=diff[t][:, a:b], func=ACT.Sigmoid)
 
         def steps_g(t):
-            nc.gpsimd.tensor_tensor(step[t][:], gate[t][:], pull[t][:], ALU.mult)
+            for a, b in HALVES:
+                nc.gpsimd.tensor_tensor(step[t][:, a:b], gate[t][:, a:b], pull[t][:, a:b], ALU.mult)
 
         for t in range(PACK - 1):
-            fetch(t, 0, S)
             fetch_a(t)
             pulls(t, 0, S)
+            steps_g(t)
             if t > 0:
                 land(t - 1, 0, S)
                 store(t - 1, 0, S)
-            steps_g(t)
         t = PACK - 1
-        at_tail = at_zb + 2048
-        tail_step = [late.tile([P, 256], F32, name="ts0", align_bytes=64, offset=at_tail)] + [
-            keep.tile([P, 128], F32, name="ts%d" % c) for c in (1, 2)
-        ]
-        tail_diff = [
-            keep.tile([P, 256], F32, name="td0"),
-            keep.tile([P, 128], F32, name="td1"),
-            late.tile([P, 128], F32, name="td2", align_bytes=64, offset=at_tail),
-        ]
-
-        def tail_gates(c):
-            a, b = CHUNKS[c]
-            nc.vector.tensor_tensor(tail_diff[c][:], picks(hw[t], l3, a, b), hb[t][:, a:b], ALU.subtract)
-            nc.scalar.activation(out=gate[t][:, a:b], in_=tail_diff[c][:], func=ACT.Sigmoid)
-
-        def tail_land(c):
-            a, b = CHUNKS[c]
-            nc.vector.tensor_tensor(tail_step[c][:], gate[t][:, a:b], pull[t][:, a:b], ALU.mult)
-            nc.vector.tensor_tensor(of[:, t, a:b], tail_step[c][:], hp[t][:, a:b], ALU.add)
-            store(t, a, b)
-            round_out(c)
-
+        tail_step = keep.tile([P, S], F32, name="tail_step")
+        tail_diff = late.tile([P, S], F32, name="tail_diff", align_bytes=64, offset=at_pull)
         for a, b in HALVES:
             fetch(t, a, b)
         pulls(t, 0, S)
-        tail_gates(0)
+        for a, b in HALVES:
+            nc.vector.tensor_tensor(tail_diff[:, a:b], picks(hw[t], l3, a, b), hb[t][:, a:b], ALU.subtract)
+            nc.scalar.activation(out=gate[t][:, a:b], in_=tail_diff[:, a:b], func=ACT.Sigmoid)
         land(t - 1, 0, S)
         store(t - 1, 0, S)
-        tail_gates(1)
-        tail_land(0)
-        tail_gates(2)
-        tail_land(1)
-        tail_land(2)
-        planes(0)
-        planes(2)
+        for a, b in HALVES:
+            nc.vector.tensor_tensor(tail_step[:, a:b], gate[t][:, a:b], pull[t][:, a:b], ALU.mult)
+        for c, (a, b) in enumerate(HALVES):
+            nc.vector.tensor_tensor(of[:, t, a:b], tail_step[:, a:b], hp[t][:, a:b], ALU.add)
+            round_out(c)
+        store(t, 0, S)
         planes(1)
+        planes(0)
         for q in range(4):
             nc.scalar.dma_start(out=out_2[0, 4 * q : 4 * q + 4, :].bitcast(I32), in_=osc[32 * q : 32 * q + 4, :].bitcast(I32))

@@ -32,16 +32,15 @@ def tile_picked_tanmix_none_po_kernel(
 
     def load_scales(queue, plane, scales, quadrants):
         for q in quadrants:
-            rows = scales[0, 4 * q : 4 * q + 4, :].bitcast(I32)
-            queue.dma_start(out=plane[32 * q : 32 * q + 32, :].bitcast(I32), in_=rows.unsqueeze(0).to_broadcast([8] + list(rows.shape)))
+            queue.dma_start(out=plane[32 * q : 32 * q + 4, :].bitcast(I32), in_=scales[0, 4 * q : 4 * q + 4, :].bitcast(I32))
 
     def picks(window, offsets, a, b):
         return window[:].indirect(offsets[:, a // LIST : b // LIST])
 
     def woven(engine_copy, dst, src):
         engine_copy(
-            out=dst[:].rearrange("p (c i t) -> p c t i", i=4, t=PACK),
-            in_=src.rearrange("p t (c i) -> p c t i", i=4),
+            out=dst[:].rearrange("p (c i t) -> p c t i", i=2, t=PACK),
+            in_=src.rearrange("p t (c i) -> p c t i", i=2),
         )
 
     with ExitStack() as ctx:
@@ -52,29 +51,25 @@ def tile_picked_tanmix_none_po_kernel(
         lists = [keep.tile([P, S // LIST], U16, name="list%d" % i) for i in range(5)]
         l_offs, l1, l2, l3, l4 = lists
         xw = late.tile([P, T], I32, name="xw", align_bytes=64, offset=0)
-        xs = keep.tile([P, T], U8, name="xs", align_bytes=64)
-        w1w = keep.tile([P, H], I32, name="w1w", align_bytes=64)
-        w1s = keep.tile([P, H], U8, name="w1s", align_bytes=64)
-        w2w = keep.tile([P, N], I32, name="w2w", align_bytes=64)
-        w2s = keep.tile([P, N], U8, name="w2s", align_bytes=64)
+        xs = late.tile([P, T], U8, name="xs", align_bytes=64, offset=4 * T + 4 * S + N)
+        ww = keep.tile([P, H], I32, name="ww", align_bytes=64)
+        ws = keep.tile([P, H], U8, name="ws", align_bytes=64)
         gain = keep.tile([P, PACK], F32, name="gain")
         warm = keep.tile([P, 8], F32, name="warm")
 
+        nc.vector.memset(xs[:].bitcast(I32), 0)
+        nc.gpsimd.memset(ws[:].bitcast(I32), 0)
         nc.vector.memset(warm[:], 0.0)
-        nc.scalar.activation(out=warm[:, 1:2], in_=warm[:, 0:1], func=ACT.Sigmoid)
 
-        nc.sync.dma_start(out=l_offs[:], in_=offs)
-        load_scales(nc.sync, xs, x_scales, range(4))
-        nc.sync.dma_start(out=w1w[:], in_=words_of(w1_words))
-        nc.sync.dma_start(out=xw[:], in_=words_of(x_words))
-        load_scales(nc.sync, w1s, w1_scales, range(4))
+        for tile, src in ((l_offs, offs), (l1, n1), (l2, n2), (l3, n3), (l4, n4)):
+            nc.sync.dma_start(out=tile[:], in_=src)
         nc.sync.dma_start(out=gain[:], in_=gn.rearrange("(p t) o -> p (t o)", t=PACK))
-        nc.sync.dma_start(out=l1[:], in_=n1)
-        nc.sync.dma_start(out=w2w[:], in_=words_of(w2_words))
-        nc.sync.dma_start(out=l2[:], in_=n2)
-        load_scales(nc.sync, w2s, w2_scales, range(4))
-        nc.sync.dma_start(out=l4[:], in_=n4)
-        nc.sync.dma_start(out=l3[:], in_=n3)
+        nc.sync.dma_start(out=ww[:], in_=words_of(w1_words))
+        nc.sync.dma_start(out=xw[:], in_=words_of(x_words))
+        load_scales(nc.scalar, xs, x_scales, range(4))
+        load_scales(nc.scalar, ws, w1_scales, range(3))
+        load_scales(nc.gpsimd, ws, w1_scales, range(3, 4))
+        nc.scalar.activation(out=warm[:, 1:2], in_=warm[:, 0:1], func=ACT.Sigmoid)
 
         def deal(dst, src, line):
             nc.vector.tensor_copy(
@@ -93,9 +88,11 @@ def tile_picked_tanmix_none_po_kernel(
         gs = keep.tile([P, S], U8, name="gs", align_bytes=64)
         nc.vector.tensor_copy(out=gs[:], in_=xs[:].indirect(l_offs[:]))
         d1w = keep.tile([P, H], I32, name="d1w", align_bytes=64)
-        d1s = keep.tile([P, H], U8, name="d1s", align_bytes=64)
-        deal(d1w, w1w, 4)
-        deal(d1s, w1s, 16)
+        d1s = late.tile([P, H], U8, name="d1s", align_bytes=64, offset=4 * T + 4 * S + N)
+        deal(d1w, ww, 4)
+        deal(d1s, ws, 16)
+        nc.sync.dma_start(out=ww[:], in_=words_of(w2_words))
+        load_scales(nc.sync, ws, w2_scales, range(4))
         w1 = (d1w, d1s)
         y = [psum.tile([P, S], F32, name="y%d" % t) for t in range(PACK)]
         for a, b in HALVES:
@@ -105,7 +102,7 @@ def tile_picked_tanmix_none_po_kernel(
             product(y[t][:], w1, t, gw[:], gs[:])
         d2w = late.tile([P, N], I32, name="d2w", align_bytes=64, offset=0)
         d2s = late.tile([P, N], U8, name="d2s", align_bytes=64, offset=4 * T + 4 * S)
-        deal(d2w, w2w, 4)
+        deal(d2w, ww, 4)
         w2 = (d2w, d2s)
 
         thw = [keep.tile([P, 2 * S], F32, name="thw%d" % t) for t in range(PACK)]
@@ -161,7 +158,7 @@ def tile_picked_tanmix_none_po_kernel(
             mix_add(t, 1)
         round_z(0)
         round_z(1)
-        deal(d2s, w2s, 16)
+        deal(d2s, ws, 16)
         for t in range(PACK):
             mix_add(t, 2)
         second(0)
@@ -173,7 +170,7 @@ def tile_picked_tanmix_none_po_kernel(
             product(hp[t][:], w2, t, zw[:], zs[:])
             nc.scalar.copy(out=h[t], in_=hp[t][:])
 
-        at_step = 4 * T + 4 * S + N
+        at_step = 5 * T + 4 * S + N
         at_pull = at_step + 4 * S
         hb_rest = [keep.tile([P, S], F32, name="hb2"), late.tile([P, S], F32, name="hb3", align_bytes=64, offset=at_step)]
         hb = [hw[1][:, S:], hw[2][:, S:], hb_rest[0][:], hb_rest[1][:]]

@@ -54,11 +54,13 @@ def tile_picked_tanmix_none_po_kernel(
         xs = late.tile([P, T], U8, name="xs", align_bytes=64, offset=4 * T + 4 * S + N)
         ww = keep.tile([P, H], I32, name="ww", align_bytes=64)
         ws = keep.tile([P, H], U8, name="ws", align_bytes=64)
+        w2s = keep.tile([P, N], U8, name="w2s", align_bytes=64)
         gain = keep.tile([P, PACK], F32, name="gain")
         warm = keep.tile([P, 8], F32, name="warm")
 
         nc.vector.memset(xs[:].bitcast(I32), 0)
         nc.gpsimd.memset(ws[:].bitcast(I32), 0)
+        nc.gpsimd.memset(w2s[:].bitcast(I32), 0)
         nc.vector.memset(warm[:], 0.0)
 
         for tile, src in ((l_offs, offs), (l1, n1), (l2, n2), (l3, n3), (l4, n4)):
@@ -69,6 +71,7 @@ def tile_picked_tanmix_none_po_kernel(
         load_scales(nc.scalar, xs, x_scales, range(4))
         load_scales(nc.scalar, ws, w1_scales, range(3))
         load_scales(nc.gpsimd, ws, w1_scales, range(3, 4))
+        load_scales(nc.gpsimd, w2s, w2_scales, range(4))
         nc.scalar.activation(out=warm[:, 1:2], in_=warm[:, 0:1], func=ACT.Sigmoid)
 
         def deal(dst, src, line):
@@ -92,7 +95,6 @@ def tile_picked_tanmix_none_po_kernel(
         deal(d1w, ww, 4)
         deal(d1s, ws, 16)
         nc.sync.dma_start(out=ww[:], in_=words_of(w2_words))
-        load_scales(nc.sync, ws, w2_scales, range(4))
         w1 = (d1w, d1s)
         y = [psum.tile([P, S], F32, name="y%d" % t) for t in range(PACK)]
         for a, b in HALVES:
@@ -101,8 +103,9 @@ def tile_picked_tanmix_none_po_kernel(
         for t in range(1, PACK):
             product(y[t][:], w1, t, gw[:], gs[:])
         d2w = late.tile([P, N], I32, name="d2w", align_bytes=64, offset=0)
-        d2s = late.tile([P, N], U8, name="d2s", align_bytes=64, offset=4 * T + 4 * S)
+        d2s = late.tile([P, N], U8, name="d2s", align_bytes=64, offset=4 * N)
         deal(d2w, ww, 4)
+        deal(d2s, w2s, 16)
         w2 = (d2w, d2s)
 
         thw = [keep.tile([P, 2 * S], F32, name="thw%d" % t) for t in range(PACK)]
@@ -158,7 +161,6 @@ def tile_picked_tanmix_none_po_kernel(
             mix_add(t, 1)
         round_z(0)
         round_z(1)
-        deal(d2s, ws, 16)
         for t in range(PACK):
             mix_add(t, 2)
         second(0)
@@ -252,4 +254,4 @@ def tile_picked_tanmix_none_po_kernel(
         planes(1)
         planes(0)
         for q in range(4):
-            nc.scalar.dma_start(out=out_2[0, 4 * q : 4 * q + 4, :].bitcast(I32), in_=osc[32 * q : 32 * q + 4, :].bitcast(I32))
+            (nc.scalar if q % 2 == 0 else nc.sync).dma_start(out=out_2[0, 4 * q : 4 * q + 4, :].bitcast(I32), in_=osc[32 * q : 32 * q + 4, :].bitcast(I32))

from contextlib import ExitStack

import concourse.mybir as mybir

K, T, S, H, N = 512, 2048, 512, 512, 512
FLOPS = 2 * K * H * S + 2 * H * N * S

F32 = mybir.dt.float32
BF16 = mybir.dt.bfloat16
I32 = mybir.dt.int32
U32 = mybir.dt.uint32
U16 = mybir.dt.uint16
U8 = mybir.dt.uint8
FP8X4 = mybir.dt.float8_e4m3fn_x4
ACT = mybir.ActivationFunctionType
ALU = mybir.AluOpType

P = 128
PACK = 4
LIST = 16
HALVES = [(0, 256), (256, 512)]
CHUNKS = [(0, 256), (256, 384), (384, 512)]


def tile_picked_tanmix_none_po_kernel(
    tc, x_words, x_scales, w1_words, w1_scales, gn, w2_words, w2_scales, offs, n1, n2, n3, n4, out_0, out_1, out_2
):
    nc = tc.nc

    def words_of(ap):
        return ap[0].rearrange("p n t -> p (n t)").bitcast(I32)

    def load_scales(queue, plane, scales, quadrants):
        for q in quadrants:
            queue.dma_start(out=plane[32 * q : 32 * q + 4, :].bitcast(I32), in_=scales[0, 4 * q : 4 * q + 4, :].bitcast(I32))

    def picks(window, offsets, a, b):
        return window[:].indirect(offsets[:, a // LIST : b // LIST])

    def woven(engine_copy, dst, src):
        engine_copy(
            out=dst[:].rearrange("p (c i t) -> p c t i", i=2, t=PACK),
            in_=src.rearrange("p t (c i) -> p c t i", i=2),
        )

    with ExitStack() as ctx:
        keep = ctx.enter_context(tc.tile_pool(name="keep", bufs=1))
        late = ctx.enter_context(tc.tile_pool(name="late", bufs=1))
        psum = ctx.enter_context(tc.psum_pool(name="psum", bufs=1))

        lists = [keep.tile([P, S // LIST], U16, name="list%d" % i) for i in range(5)]
        l_offs, l1, l2, l3, l4 = lists
        xw = late.tile([P, T], I32, name="xw", align_bytes=64, offset=0)
        xs = late.tile([P, T], U8, name="xs", align_bytes=64, offset=4 * T + 4 * S + N)
        ww = keep.tile([P, H], I32, name="ww", align_bytes=64)
        ws = keep.tile([P, H], U8, name="ws", align_bytes=64)
        w2s = keep.tile([P, N], U8, name="w2s", align_bytes=64)
        gain = keep.tile([P, PACK], F32, name="gain")
        warm = keep.tile([P, 8], F32, name="warm")

        nc.vector.memset(xs[:].bitcast(I32), 0)
        nc.gpsimd.memset(ws[:].bitcast(I32), 0)
        nc.gpsimd.memset(w2s[:].bitcast(I32), 0)
        nc.vector.memset(warm[:], 0.0)

        for tile, src in ((l_offs, offs), (l1, n1), (l2, n2), (l3, n3), (l4, n4)):
            nc.sync.dma_start(out=tile[:], in_=src)
        nc.sync.dma_start(out=gain[:], in_=gn.rearrange("(p t) o -> p (t o)", t=PACK))
        nc.sync.dma_start(out=ww[:], in_=words_of(w1_words))
        nc.sync.dma_start(out=xw[:], in_=words_of(x_words))
        load_scales(nc.scalar, xs, x_scales, range(4))
        load_scales(nc.scalar, ws, w1_scales, range(3))
        load_scales(nc.gpsimd, ws, w1_scales, range(3, 4))
        load_scales(nc.gpsimd, w2s, w2_scales, range(4))
        nc.scalar.activation(out=warm[:, 1:2], in_=warm[:, 0:1], func=ACT.Sigmoid)

        def deal(dst, src, line):
            nc.vector.tensor_copy(
                out=dst[:].rearrange("p (t c i) -> p c t i", t=PACK, i=line),
                in_=src[:].rearrange("p (c i t) -> p c t i", t=PACK, i=line),
            )

        def product(bank, w, t, codes, scales):
            cols = slice(t * P, (t + 1) * P)
            nc.tensor.matmul_mx(
                out=bank, lhsT=w[0][:, cols].bitcast(FP8X4), lhsT_scale=w[1][:, cols],
                rhs=codes.bitcast(FP8X4), rhs_scale=scales, start=True, stop=True,
            )

        gw = keep.tile([P, S], U32, name="gw", align_bytes=64)
        gs = keep.tile([P, S], U8, name="gs", align_bytes=64)
        nc.vector.tensor_copy(out=gs[:], in_=xs[:].indirect(l_offs[:]))
        d1w = keep.tile([P, H], I32, name="d1w", align_bytes=64)
        d1s = late.tile([P, H], U8, name="d1s", align_bytes=64, offset=4 * T + 4 * S + N)
        deal(d1w, ww, 4)
        deal(d1s, ws, 16)
        nc.sync.dma_start(out=ww[:], in_=words_of(w2_words))
        w1 = (d1w, d1s)
        y = [psum.tile([P, S], F32, name="y%d" % t) for t in range(PACK)]
        for a, b in HALVES:
            nc.vector.tensor_copy(out=gw[:, a:b], in_=xw[:].bitcast(U32).indirect(l_offs[:, a // LIST : b // LIST]))
            product(y[0][:, a:b], w1, 0, gw[:, a:b], gs[:, a:b])
        for t in range(1, PACK):
            product(y[t][:], w1, t, gw[:], gs[:])
        d2w = late.tile([P, N], I32, name="d2w", align_bytes=64, offset=0)
        d2s = late.tile([P, N], U8, name="d2s", align_bytes=64, offset=4 * N)
        deal(d2w, ww, 4)
        deal(d2s, w2s, 16)
        w2 = (d2w, d2s)

        thw = [keep.tile([P, 2 * S], F32, name="thw%d" % t) for t in range(PACK)]
        gth_last = late.tile([P, S + N // 4], F32, name="gth_last", align_bytes=64, offset=4 * T)
        th = [w[:, :S] for w in thw]
        gth = [w[:, S:] for w in thw[1:]] + [gth_last[:, :S]]
        nc.vector.memset(thw[0][:, S:], 0.0)
        hth = [keep.tile([P, S], F32, name="hth%d" % t) for t in range(PACK)]
        prod = [keep.tile([P, S], F32, name="prod%d" % t) for t in range(PACK)]
        zf = [
            keep.tile([P, PACK, 256], F32, name="zf0"),
            keep.tile([P, PACK, 128], F32, name="zf1"),
            late.tile([P, PACK, 128], F32, name="zf2", align_bytes=64, offset=4 * T),
        ]
        zb = [keep.tile([P, PACK * (b - a)], BF16, name="zb%d" % c, align_bytes=64) for c, (a, b) in enumerate(CHUNKS)]
        zw = keep.tile([P, S], U32, name="zw", align_bytes=64)
        zs = keep.tile([P, S], U8, name="zs", align_bytes=64)
        hp = [psum.tile([P, S], F32, name="hp%d" % t) for t in range(PACK)]
        hw = [keep.tile([P, 2 * S if t < PACK - 1 else S], F32, name="hw%d" % t) for t in range(PACK)]
        h = [w[:, :S] for w in hw]
        nc.vector.memset(hw[0][:, S:], 0.0)

        def tables(t, parts):
            for a, b in parts:
                nc.scalar.activation(out=th[t][:, a:b], in_=y[t][:, a:b], func=ACT.Tanh)
                nc.scalar.activation(out=gth[t][:, a:b], in_=th[t][:, a:b], func=ACT.Copy, scale=gain[:, t : t + 1])
            nc.scalar.activation(out=hth[t][:], in_=gth[t], func=ACT.Copy, scale=-0.5)

        def mix_mul(t, a, b):
            nc.vector.tensor_tensor(prod[t][:, a:b], picks(thw[t], l1, a, b), gth[t][:, a:b], ALU.mult)

        def mix_add(t, c):
            a, b = CHUNKS[c]
            nc.vector.tensor_tensor(zf[c][:, t, :], picks(hth[t], l2, a, b), prod[t][:, a:b], ALU.add)

        def round_z(c):
            woven(nc.vector.tensor_copy if c == len(CHUNKS) - 1 else nc.scalar.copy, zb[c], zf[c][:])

        def second(c):
            a, b = CHUNKS[c]
            nc.vector.quantize_mx(out=zw[:, a:b].bitcast(FP8X4), scales=zs[:, a:b], in_=zb[c][:])
            product(hp[0][:, a:b], w2, 0, zw[:, a:b], zs[:, a:b])

        for t in range(PACK):
            tables(t, HALVES if t == 0 else [(0, S)])
        for t in range(PACK):
            if t == 0:
                for a, b in HALVES:
                    mix_mul(t, a, b)
            else:
                mix_mul(t, 0, S)
            mix_add(t, 0)
            mix_add(t, 1)
        round_z(0)
        round_z(1)
        for t in range(PACK):
            mix_add(t, 2)
        second(0)
        round_z(2)
        second(1)
        second(2)
        nc.scalar.copy(out=h[0], in_=hp[0][:])
        for t in range(1, PACK):
            product(hp[t][:], w2, t, zw[:], zs[:])
            nc.scalar.copy(out=h[t], in_=hp[t][:])

        at_step = 5 * T + 4 * S + N
        at_pull = at_step + 4 * S
        hb_rest = [keep.tile([P, S], F32, name="hb2"), late.tile([P, S], F32, name="hb3", align_bytes=64, offset=at_step)]
        hb = [hw[1][:, S:], hw[2][:, S:], hb_rest[0][:], hb_rest[1][:]]
        ha = [keep.tile([P, S], F32, name="ha%d" % t) for t in range(PACK - 1)]
        diff = [keep.tile([P, S], F32, name="diff%d" % t) for t in range(PACK - 1)]
        gate = [keep.tile([P, S], F32, name="gate%d" % t) for t in range(PACK)]
        pull = [
            late.tile([P, S], F32, name="pull2", align_bytes=64, offset=at_pull) if t == 2 else keep.tile([P, S], F32, name="pull%d" % t)
            for t in range(PACK)
        ]
        step = [
            late.tile([P, S], F32, name="step1", align_bytes=64, offset=at_step) if t == 1 else keep.tile([P, S], F32, name="step%d" % t)
            for t in range(PACK - 1)
        ]
        of = keep.tile([P, PACK, S], F32, name="of")
        ob = [keep.tile([P, PACK * (b - a)], BF16, name="ob%d" % c, align_bytes=64) for c, (a, b) in enumerate(HALVES)]
        ow = keep.tile([P, S], I32, name="ow", align_bytes=64)
        osc = keep.tile([P, S], U8, name="osc", align_bytes=64)
        out_rows = out_0.rearrange("(p t) s -> p t s", t=PACK)
        out_words = words_of(out_1)

        def fetch(t, a, b):
            nc.vector.tensor_copy(out=hb[t][:, a:b], in_=picks(hw[t], l4, a, b))

        def pulls(t, a, b):
            nc.vector.tensor_tensor(pull[t][:, a:b], hb[t][:, a:b], hp[t][:, a:b], ALU.subtract)

        def land(t, a, b):
            nc.vector.tensor_tensor(of[:, t, a:b], step[t][:, a:b], hp[t][:, a:b], ALU.add)

        def store(t, a, b):
            nc.sync.dma_start(out=out_rows[:, t, a:b], in_=of[:, t, a:b])

        def round_out(c):
            a, b = HALVES[c]
            woven(nc.vector.tensor_copy if c == len(HALVES) - 1 else nc.scalar.copy, ob[c], of[:, :, a:b])

        def planes(c):
            a, b = HALVES[c]
            nc.vector.quantize_mx(out=ow[:, a:b].bitcast(FP8X4), scales=osc[:, a:b], in_=ob[c][:])
            nc.sync.dma_start(out=out_words[:, a:b], in_=ow[:, a:b])

        def fetch_a(t):
            for a, b in HALVES if t < 2 else [(0, S)]:
                fetch(t, a, b)
                nc.vector.tensor_copy(out=ha[t][:, a:b], in_=picks(hw[t], l3, a, b))
            for a, b in HALVES:
                nc.gpsimd.tensor_tensor(diff[t][:, a:b], ha[t][:, a:b], hb[t][:, a:b], ALU.subtract)
                nc.scalar.activation(out=gate[t][:, a:b], in_=diff[t][:, a:b], func=ACT.Sigmoid)

        def steps_g(t):
            for a, b in HALVES:
                nc.gpsimd.tensor_tensor(step[t][:, a:b], gate[t][:, a:b], pull[t][:, a:b], ALU.mult)

        for t in range(PACK - 1):
            fetch_a(t)
            pulls(t, 0, S)
            steps_g(t)
            if t > 0:
                land(t - 1, 0, S)
                store(t - 1, 0, S)
        t = PACK - 1
        tail_step = keep.tile([P, S], F32, name="tail_step")
        tail_diff = late.tile([P, S], F32, name="tail_diff", align_bytes=64, offset=at_pull)
        for a, b in HALVES:
            fetch(t, a, b)
        pulls(t, 0, S)
        for a, b in HALVES:
            nc.vector.tensor_tensor(tail_diff[:, a:b], picks(hw[t], l3, a, b), hb[t][:, a:b], ALU.subtract)
            nc.scalar.activation(out=gate[t][:, a:b], in_=tail_diff[:, a:b], func=ACT.Sigmoid)
        land(t - 1, 0, S)
        store(t - 1, 0, S)
        for a, b in HALVES:
            nc.vector.tensor_tensor(tail_step[:, a:b], gate[t][:, a:b], pull[t][:, a:b], ALU.mult)
        for c, (a, b) in enumerate(HALVES):
            nc.vector.tensor_tensor(of[:, t, a:b], tail_step[:, a:b], hp[t][:, a:b], ALU.add)
            round_out(c)
        store(t, 0, S)
        planes(1)
        planes(0)
        for q in range(4):
            (nc.scalar if q % 2 == 0 else nc.sync).dma_start(out=out_2[0, 4 * q : 4 * q + 4, :].bitcast(I32), in_=osc[32 * q : 32 * q + 4, :].bitcast(I32))
